import numpy as np
import ml_dtypes


def mxq(x, axis, fmt="e4m3"):
    dtype, down = {"e4m3": (ml_dtypes.float8_e4m3fn, 7), "e5m2": (ml_dtypes.float8_e5m2, 14)}[fmt]
    v = np.moveaxis(np.asarray(x, np.float32).astype(ml_dtypes.bfloat16).astype(np.float64), axis, -1)
    blocks = v.reshape(v.shape[:-1] + (-1, 32))
    amax = np.abs(blocks).max(-1, keepdims=True)
    byte = np.maximum(np.where(amax > 0, np.frexp(amax)[1] - 1 + 127, 0) - down, 1)
    scale = np.exp2(byte - 127.0)
    codes = (blocks / scale).astype(np.float32).astype(dtype).astype(np.float64)
    return np.moveaxis((codes * scale).reshape(v.shape), -1, axis)


WIDE = False


def mx_kscale(k):
    if not WIDE:
        return np.ones(k)
    levels = np.array([30, -30])
    if k % 512:
        return np.exp2(np.random.permutation(np.resize(levels, k // 32))).repeat(32)
    a = np.empty((k // 512, 16))
    for p in range(k // 512):
        a[p, :8] = np.random.permutation(np.resize(levels, 8))
        for g in range(8):
            far = levels[np.abs(levels - a[p, g]) >= 10]
            a[p, g + 8] = far[np.random.randint(len(far))]
    return np.exp2(a.ravel()).repeat(32)


BF16 = ml_dtypes.bfloat16


def bf(x):
    return np.asarray(x, np.float32).astype(BF16)


def f64(x):
    return np.asarray(x).astype(np.float64)


B, P, D = 4, 512, 1024


def sigmoid(v):
    return 1.0 / (1.0 + np.exp(-v))


def gelu(v):
    return 0.5 * v * (1.0 + np.tanh(0.7978845608028654 * (v + 0.044715 * v * v * v)))


def setup_inputs():
    s, t = mx_kscale(P), mx_kscale(D)
    rn = np.random.standard_normal
    return {"x": bf(rn((B, P, D))),
            "alpha": bf((1 + 0.1 * rn(P)) * s),
            "beta": bf(0.3 * rn(P) * s),
            "wa": bf(rn((P, P)) / np.sqrt(P) / s[:, None]),
            "ba": bf(0.3 * rn(P)),
            "wg": bf(rn((P, P)) / np.sqrt(P) / s[:, None]),
            "bg": bf(0.3 * rn(P)),
            "gamma": bf((1 + 0.1 * rn(D)) * t),
            "delta": bf(0.3 * rn(D) * t),
            "wc": bf(1.5 * rn((D, D)) / np.sqrt(D) / t[:, None]),
            "bc": bf(0.3 * rn(D))}


def reference(x, alpha, beta, wa, ba, wg, bg, gamma, delta, wc, bc):
    xp = f64(x).transpose(1, 0, 2).reshape(P, B * D)
    v = mxq(xp * f64(alpha)[:, None] + f64(beta)[:, None], 0, "e4m3")
    a = (mxq(f64(wa), 0, "e4m3").T @ v) + f64(ba)[:, None]
    g = (mxq(f64(wg), 0, "e4m3").T @ v) + f64(bg)[:, None]
    u = xp + a * sigmoid(g)
    u = u.reshape(P, B, D).transpose(1, 0, 2).reshape(B * P, D)
    h = u * f64(gamma) + f64(delta)
    z = (mxq(h, 1, "e5m2") @ mxq(f64(wc), 0, "e4m3")) + f64(bc)
    return (u + gelu(z)).reshape(B, P, D)

@@ -1,0 +1,258 @@
+from contextlib import ExitStack
+
+import concourse.mybir as mybir
+from concourse.masks import make_identity
+
+B, NP, D = 4, 512, 1024
+P = 128
+T = 4
+H = 512
+G = D // H
+
+F32 = mybir.dt.float32
+BF16 = mybir.dt.bfloat16
+U32 = mybir.dt.uint32
+U8 = mybir.dt.uint8
+E4M3 = mybir.dt.float8_e4m3fn_x4
+E5M2 = mybir.dt.float8_e5m2_x4
+ALU = mybir.AluOpType
+ACT = mybir.ActivationFunctionType
+
+FLOPS = 2 * 2 * B * D * NP * NP + 2 * B * NP * D * D
+
+
+def tile_patch_channel_mixer_f3_kernel(tc, x, alpha, beta, wa, ba, wg, bg, gamma, delta, wc, bc, out):
+    nc = tc.nc
+    with ExitStack() as ctx:
+        keep = ctx.enter_context(tc.tile_pool(name="keep", bufs=1))
+        work = ctx.enter_context(tc.tile_pool(name="work", bufs=2))
+        psum = ctx.enter_context(tc.psum_pool(name="psum", bufs=1))
+
+        par_p = keep.tile([P, 4, 16], BF16, name="par_p")
+        par_d = keep.tile([P, 3, 16], BF16, name="par_d")
+        xs = [None] * B
+
+        def load_x(i):
+            xs[i] = work.tile([P, T, D], BF16, name="x_sb", tag="x_sb", bufs=3)
+            return xs[i]
+
+        x0 = load_x(0)
+        xv = [x[i].rearrange("(p t) d -> p t d", t=T) for i in range(B)]
+        nc.sync.dma_start(out=x0[:, :, 0:H], in_=xv[0][:, :, 0:H])
+        raws = []
+        for w in (wa, wg):
+            raw = work.tile([P, T, NP], BF16, name="raw", tag="raw", bufs=3)
+            nc.sync.dma_start(out=raw[:], in_=w.rearrange("(p j) c -> p j c", j=T))
+            raws.append(raw)
+        for s, vec in enumerate((alpha, beta, ba, bg)):
+            nc.scalar.dma_start(out=par_p[:, s, 0:T], in_=vec.rearrange("(p t) -> p t", t=T))
+        for s, vec in enumerate((gamma, delta, bc)):
+            nc.scalar.dma_start(
+                out=par_d[:, s, 0 : G * T].rearrange("p (g t) -> p g t", t=T),
+                in_=vec.rearrange("(g p t) -> p g t", g=G, t=T),
+            )
+        nc.sync.dma_start(out=x0[:, :, H:D], in_=xv[0][:, :, H:D])
+
+        ident = keep.tile([P, P], F32, name="ident")
+        make_identity(nc, ident[:])
+        pp = keep.tile([P, 4, T], F32, name="pp")
+        pd = keep.tile([P, 3, G * T], F32, name="pd")
+        nc.vector.tensor_copy(out=pp[:], in_=par_p[:, :, 0:T])
+        nc.vector.tensor_copy(out=pd[:], in_=par_d[:, :, 0 : G * T])
+
+        def col(s, t):
+            return pp[:, s, t : t + 1]
+
+        def dcol(s, q):
+            return pd[:, s, q : q + 1]
+
+        def quant(src, codes, scales, fmt):
+            nc.vector.quantize_mx(out=codes.bitcast(fmt), scales=scales, in_=src)
+
+        def weight_block(raw, codes, scales, eng):
+            inter = work.tile([P, H * T], BF16, name="inter", tag="inter", bufs=4, align_bytes=64)
+            d = inter[:].rearrange("p (t m j) -> p t m j", t=T, j=T)
+            s = raw[:].rearrange("p j (m t) -> p t m j", t=T)
+            if eng == "s":
+                nc.scalar.copy(out=d, in_=s)
+            else:
+                nc.vector.tensor_copy(out=d, in_=s)
+            quant(inter[:], codes, scales, E4M3)
+
+        w_codes = keep.tile([P, 2, NP], U32, name="w_codes", align_bytes=64)
+        w_scales = keep.tile([P, 2, NP], U8, name="w_scales", align_bytes=64)
+        c_codes = keep.tile([P, G, D], U32, name="c_codes", align_bytes=64)
+        c_scales = keep.tile([P, G, D], U8, name="c_scales", align_bytes=64)
+
+        vas = [None] * B
+        vq = {}
+
+        def affine_v(i, halves):
+            if vas[i] is None:
+                vas[i] = work.tile([P, T, D], BF16, name="va", tag="va", bufs=2)
+            lo, hi = halves[0] * H, (halves[-1] + 1) * H
+            for t in range(T):
+                nc.vector.tensor_scalar(
+                    out=vas[i][:, t, lo:hi], in0=xs[i][:, t, lo:hi],
+                    scalar1=col(0, t), scalar2=col(1, t), op0=ALU.mult, op1=ALU.add,
+                )
+
+        def quant_v(i, g, eng):
+            inter = work.tile([P, H * T], BF16, name="inter", tag="inter", bufs=4, align_bytes=64)
+            d = inter[:].rearrange("p (c t) -> p c t", t=T)
+            s = vas[i][:, :, g * H : (g + 1) * H].rearrange("p t c -> p c t")
+            if eng == "s":
+                nc.scalar.copy(out=d, in_=s)
+            else:
+                nc.vector.tensor_copy(out=d, in_=s)
+            codes = work.tile([P, H], U32, name="v_codes", tag="v_codes", bufs=3, align_bytes=64)
+            scales = work.tile([P, H], U8, name="v_scales", tag="v_scales", bufs=3, align_bytes=64)
+            quant(inter[:], codes[:], scales[:], E4M3)
+            vq[i, g] = (codes, scales)
+
+        us = [None] * B
+
+        def stage1(i, g, m, add_eng):
+            codes, scales = vq[i, g]
+            pa = psum.tile([P, H], F32, name="pa", tag="pa", bufs=2)
+            pg = psum.tile([P, H], F32, name="pg", tag="pg", bufs=2)
+            for k, bank in ((1, pg), (0, pa)):
+                nc.tensor.matmul_mx(
+                    out=bank[:],
+                    lhsT=w_codes[:, k, m * P : (m + 1) * P].bitcast(E4M3),
+                    lhsT_scale=w_scales[:, k, m * P : (m + 1) * P],
+                    rhs=codes[:].bitcast(E4M3), rhs_scale=scales[:],
+                    start=True, stop=True,
+                )
+            sg = work.tile([P, T, P], F32, name="sg", tag="sg", bufs=3)
+            nc.scalar.activation(
+                out=sg[:], in_=pg[:].rearrange("p (q t) -> p t q", t=T), func=ACT.Sigmoid, bias=col(3, m)
+            )
+            tt = work.tile([P, T, P], F32, name="tt", tag="tt", bufs=3)
+            nc.vector.scalar_tensor_tensor(
+                out=tt[:], in0=pa[:].rearrange("p (q t) -> p t q", t=T), scalar=col(2, m), in1=sg[:],
+                op0=ALU.add, op1=ALU.mult,
+            )
+            if us[i] is None:
+                us[i] = work.tile([P, T, G, T, P], F32, name="u", tag="u", bufs=4)
+            xin = xs[i][:, m, g * H : (g + 1) * H].rearrange("p (q t) -> p t q", t=T)
+            eng = nc.gpsimd if add_eng == "g" else nc.vector
+            eng.tensor_tensor(out=us[i][:, m, g, :, :], in0=tt[:], in1=xin, op=ALU.add)
+
+        has = {}
+
+        def trans_h(i, g, copy_eng):
+            ha = work.tile([P, T, H], BF16, name="ha", tag="ha", bufs=2)
+            for t in range(T):
+                bank = psum.tile([P, T, P], F32, name="pt", tag="pt", bufs=4)
+                for m in range(T):
+                    nc.tensor.transpose(bank[:, m, :], us[i][:, m, g, t, :], ident[:])
+                q = g * T + t
+                if copy_eng[t] == "s":
+                    nc.scalar.activation(
+                        out=ha[:, t, :], in_=bank[:].rearrange("p m c -> p (m c)"), func=ACT.Identity,
+                        scale=dcol(0, q), bias=dcol(1, q),
+                    )
+                else:
+                    nc.vector.tensor_scalar(
+                        out=ha[:, t, :], in0=bank[:].rearrange("p m c -> p (m c)"),
+                        scalar1=dcol(0, q), scalar2=dcol(1, q), op0=ALU.mult, op1=ALU.add,
+                    )
+            has[i, g] = ha
+
+        hq = {}
+
+        def quant_h(i, g):
+            inter = work.tile([P, H * T], BF16, name="inter", tag="inter", bufs=4, align_bytes=64)
+            nc.vector.tensor_copy(
+                out=inter[:].rearrange("p (c t) -> p c t", t=T), in_=has[i, g][:].rearrange("p t c -> p c t")
+            )
+            codes = work.tile([P, H], U32, name="h_codes", tag="h_codes", bufs=8, align_bytes=64)
+            scales = work.tile([P, H], U8, name="h_scales", tag="h_scales", bufs=8, align_bytes=64)
+            quant(inter[:], codes[:], scales[:], E5M2)
+            hq[i, g] = (codes, scales)
+
+        ges = {}
+
+        def stage2(i, f, t):
+            q = f * T + t
+            bank = psum.tile([P, H], F32, name="pz", tag="pa" if t % 2 else "pg", bufs=2)
+            for g in range(G):
+                codes, scales = hq[i, g]
+                nc.tensor.matmul_mx(
+                    out=bank[:],
+                    lhsT=c_codes[:, g, q * P : (q + 1) * P].bitcast(E4M3),
+                    lhsT_scale=c_scales[:, g, q * P : (q + 1) * P],
+                    rhs=codes[:].bitcast(E5M2), rhs_scale=scales[:],
+                    start=(g == 0), stop=(g == G - 1),
+                )
+            ge = work.tile([P, H], F32, name="ge", tag="ge", bufs=8)
+            nc.scalar.activation(out=ge[:], in_=bank[:], func=ACT.Gelu_apprx_tanh, bias=dcol(2, q))
+            ges[i, f, t] = ge
+
+        def finish(i, f):
+            res = work.tile([P, T, H], F32, name="res", tag="res", bufs=2)
+            ov = out[i].rearrange("(p t) d -> p t d", t=T)
+            for m in range(T):
+                bank = psum.tile([P, T, P], F32, name="pt", tag="pt", bufs=4)
+                for t in range(T):
+                    nc.tensor.transpose(bank[:, t, :], ges[i, f, t][:, m * P : (m + 1) * P], ident[:])
+                nc.vector.tensor_tensor(
+                    out=res[:, m, :].rearrange("p (q t) -> p q t", t=T),
+                    in0=bank[:].rearrange("p t q -> p q t"),
+                    in1=us[i][:, m, f, :, :].rearrange("p t q -> p q t"),
+                    op=ALU.add,
+                )
+                if m % 2:
+                    nc.sync.dma_start(
+                        out=ov[:, m - 1 : m + 1, f * H : (f + 1) * H], in_=res[:, m - 1 : m + 1, :]
+                    )
+
+        for i in range(1, B - 1):
+            pass
+        affine_v(0, (0,))
+        for k in range(2):
+            weight_block(raws[k], w_codes[:, k, :], w_scales[:, k, :], "sv"[k])
+        quant_v(0, 0, "v")
+        load_x(1)
+        nc.sync.dma_start(out=xs[1][:], in_=xv[1])
+        affine_v(0, (1,))
+        quant_v(0, 1, "v")
+
+        wc_raw = []
+        for g in range(G):
+            for f in range(G):
+                raw = work.tile([P, T, NP], BF16, name="raw", tag="raw", bufs=3)
+                src = wc[g * H : (g + 1) * H, f * H : (f + 1) * H]
+                nc.sync.dma_start(out=raw[:], in_=src.rearrange("(p j) c -> p j c", j=T))
+                wc_raw.append((g, f, raw))
+
+        units = [(i, g) for i in range(B) for g in range(G)]
+        for n, (i, g) in enumerate(units):
+            if g == 0 and i + 2 < B:
+                load_x(i + 2)
+                nc.sync.dma_start(out=xs[i + 2][:], in_=xv[i + 2])
+            if g == 0 and i + 1 < B:
+                affine_v(i + 1, (0, 1))
+            for m in range(T):
+                stage1(i, g, m, "v")
+                if m == 1 and i + 1 < B:
+                    quant_v(i + 1, g, "s")
+            if n < 4:
+                cg, cf, raw = wc_raw[n]
+                weight_block(
+                    raw, c_codes[:, cg, cf * H : (cf + 1) * H], c_scales[:, cg, cf * H : (cf + 1) * H], "v"
+                )
+            if n >= 1:
+                trans_h(*units[n - 1], "ssss")
+            if n >= 2:
+                quant_h(*units[n - 2])
+        trans_h(*units[-1], "svsv")
+        quant_h(*units[-2])
+        quant_h(*units[-1])
+        for n, (i, f) in enumerate(units):
+            for t in range(T):
+                stage2(i, f, t)
+            if n >= 1:
+                finish(*units[n - 1])
+        finish(*units[-1])

@@ -18,6 +18,22 @@ E5M2 = mybir.dt.float8_e5m2_x4
 ALU = mybir.AluOpType
 ACT = mybir.ActivationFunctionType
 
+L_OT = 40
+L_Z = 36
+L_M = 0
+L_HI = 8
+R = 4
+MAN = {mybir.EngineType.PE}
+WC_ENG = "vvvv"
+NAT = "vvvv"
+WC_AT = 1
+HI = "vvvv"
+HP = 2
+HW = "vsvs"
+V0 = "vsvv"
+L_HT = 4
+VI = "sssv"
+HC = "ssss"
 FLOPS = 2 * 2 * B * D * NP * NP + 2 * B * NP * D * D
 
 
@@ -29,36 +45,45 @@ def tile_patch_channel_mixer_f3_kernel(tc, x, alpha, beta, wa, ba, wg, bg, gamma
         psum = ctx.enter_context(tc.psum_pool(name="psum", bufs=1))
 
         par_p = keep.tile([P, 4, 16], BF16, name="par_p")
-        par_d = keep.tile([P, 3, 16], BF16, name="par_d")
-        xs = [None] * B
-
-        def load_x(i):
-            xs[i] = work.tile([P, T, D], BF16, name="x_sb", tag="x_sb", bufs=3)
-            return xs[i]
-
-        x0 = load_x(0)
-        xv = [x[i].rearrange("(p t) d -> p t d", t=T) for i in range(B)]
-        nc.sync.dma_start(out=x0[:, :, 0:H], in_=xv[0][:, :, 0:H])
-        raws = []
-        for w in (wa, wg):
-            raw = work.tile([P, T, NP], BF16, name="raw", tag="raw", bufs=3)
-            nc.sync.dma_start(out=raw[:], in_=w.rearrange("(p j) c -> p j c", j=T))
-            raws.append(raw)
+        par_d = keep.tile([P, 2, 16], BF16, name="par_d")
         for s, vec in enumerate((alpha, beta, ba, bg)):
             nc.scalar.dma_start(out=par_p[:, s, 0:T], in_=vec.rearrange("(p t) -> p t", t=T))
-        for s, vec in enumerate((gamma, delta, bc)):
+        bc_rows = keep.tile([P, P], BF16, name="bc_rows", align_bytes=64)
+        nc.gpsimd.memset(bc_rows[:], 0.0)
+        nc.scalar.dma_start(out=bc_rows[0 : G * T, :], in_=bc.rearrange("(q p) -> q p", p=P))
+        for s, vec in enumerate((gamma, delta)):
             nc.scalar.dma_start(
                 out=par_d[:, s, 0 : G * T].rearrange("p (g t) -> p g t", t=T),
                 in_=vec.rearrange("(g p t) -> p g t", g=G, t=T),
             )
+        xs = [None] * B
+
+        def load_x(i):
+            xs[i] = work.tile([P, T, D], BF16, name="x_sb", tag="x_sb", bufs=4)
+            return xs[i]
+
+        x0 = load_x(0)
+        xv = [x[i].rearrange("(p t) d -> p t d", t=T) for i in range(B)]
+        raws = []
+        for w in (wg, wa):
+            raw = work.tile([P, T, NP], BF16, name="raw", tag="raw", bufs=3)
+            nc.sync.dma_start(out=raw[:], in_=w.rearrange("(p j) c -> p j c", j=T))
+            raws.append(raw)
+            if w is wg:
+                nc.sync.dma_start(out=x0[:, :, 0:H], in_=xv[0][:, :, 0:H])
         nc.sync.dma_start(out=x0[:, :, H:D], in_=xv[0][:, :, H:D])
 
         ident = keep.tile([P, P], F32, name="ident")
         make_identity(nc, ident[:])
+        ident_bf = keep.tile([P, P], BF16, name="ident_bf")
+        make_identity(nc, ident_bf[:])
         pp = keep.tile([P, 4, T], F32, name="pp")
         pd = keep.tile([P, 3, G * T], F32, name="pd")
         nc.vector.tensor_copy(out=pp[:], in_=par_p[:, :, 0:T])
-        nc.vector.tensor_copy(out=pd[:], in_=par_d[:, :, 0 : G * T])
+        nc.vector.tensor_copy(out=pd[:, 0:2, :], in_=par_d[:, :, 0 : G * T])
+        bc_t = psum.tile([P, P], BF16, name="bc_t", tag="pt", bufs=4)
+        nc.tensor.transpose(bc_t[:], bc_rows[:], ident_bf[:])
+        nc.vector.tensor_copy(out=pd[:, 2, :], in_=bc_t[:, 0 : G * T])
 
         def col(s, t):
             return pp[:, s, t : t + 1]
@@ -69,15 +94,27 @@ def tile_patch_channel_mixer_f3_kernel(tc, x, alpha, beta, wa, ba, wg, bg, gamma
         def quant(src, codes, scales, fmt):
             nc.vector.quantize_mx(out=codes.bitcast(fmt), scales=scales, in_=src)
 
-        def weight_block(raw, codes, scales, eng):
-            inter = work.tile([P, H * T], BF16, name="inter", tag="inter", bufs=4, align_bytes=64)
-            d = inter[:].rearrange("p (t m j) -> p t m j", t=T, j=T)
-            s = raw[:].rearrange("p j (m t) -> p t m j", t=T)
+        winter = {}
+
+        def weight_part(key, raw, t, eng, natural=False):
+            if t == 0:
+                winter[key] = work.tile([P, H * T], BF16, name="inter", tag="inter", bufs=5, align_bytes=64)
+            d = winter[key][:].rearrange("p (t m j) -> p t m j", t=T, j=T)[:, t]
+            s = raw[:].rearrange("p j (t m) -> p t m j" if natural else "p j (m t) -> p t m j", t=T)[:, t]
             if eng == "s":
                 nc.scalar.copy(out=d, in_=s)
+            elif eng == "g":
+                nc.gpsimd.tensor_scalar(out=d, in0=s, scalar1=1.0, scalar2=0.0, op0=ALU.mult, op1=ALU.add)
             else:
                 nc.vector.tensor_copy(out=d, in_=s)
-            quant(inter[:], codes, scales, E4M3)
+
+        def weight_quant(key, codes, scales):
+            quant(winter[key][:], codes, scales, E4M3)
+
+        def weight_block(raw, codes, scales, eng):
+            for t in range(T):
+                weight_part("w", raw, t, eng[t])
+            weight_quant("w", codes, scales)
 
         w_codes = keep.tile([P, 2, NP], U32, name="w_codes", align_bytes=64)
         w_scales = keep.tile([P, 2, NP], U8, name="w_scales", align_bytes=64)
@@ -85,37 +122,42 @@ def tile_patch_channel_mixer_f3_kernel(tc, x, alpha, beta, wa, ba, wg, bg, gamma
         c_scales = keep.tile([P, G, D], U8, name="c_scales", align_bytes=64)
 
         vas = [None] * B
+        vin = {}
         vq = {}
 
-        def affine_v(i, halves):
+        def affine_v(i, t, lo=0, hi=D):
             if vas[i] is None:
                 vas[i] = work.tile([P, T, D], BF16, name="va", tag="va", bufs=2)
-            lo, hi = halves[0] * H, (halves[-1] + 1) * H
-            for t in range(T):
-                nc.vector.tensor_scalar(
-                    out=vas[i][:, t, lo:hi], in0=xs[i][:, t, lo:hi],
-                    scalar1=col(0, t), scalar2=col(1, t), op0=ALU.mult, op1=ALU.add,
-                )
+            nc.vector.tensor_scalar(
+                out=vas[i][:, t, lo:hi], in0=xs[i][:, t, lo:hi],
+                scalar1=col(0, t), scalar2=col(1, t), op0=ALU.mult, op1=ALU.add,
+            )
 
-        def quant_v(i, g, eng):
-            inter = work.tile([P, H * T], BF16, name="inter", tag="inter", bufs=4, align_bytes=64)
-            d = inter[:].rearrange("p (c t) -> p c t", t=T)
-            s = vas[i][:, :, g * H : (g + 1) * H].rearrange("p t c -> p c t")
+        def inter_v(i, g, part, parts, eng):
+            if part == 0:
+                vin[i, g] = work.tile([P, H * T], BF16, name="inter", tag="inter", bufs=5, align_bytes=64)
+            w = H // parts
+            lo = part * w
+            d = vin[i, g][:, lo * T : (lo + w) * T].rearrange("p (c k t) -> p c t k", k=4, t=T)
+            s = vas[i][:, :, g * H + lo : g * H + lo + w].rearrange("p t (c k) -> p c t k", k=4)
             if eng == "s":
                 nc.scalar.copy(out=d, in_=s)
             else:
                 nc.vector.tensor_copy(out=d, in_=s)
+
+        def quant_v(i, g):
             codes = work.tile([P, H], U32, name="v_codes", tag="v_codes", bufs=3, align_bytes=64)
             scales = work.tile([P, H], U8, name="v_scales", tag="v_scales", bufs=3, align_bytes=64)
-            quant(inter[:], codes[:], scales[:], E4M3)
+            quant(vin[i, g][:], codes[:], scales[:], E4M3)
             vq[i, g] = (codes, scales)
 
         us = [None] * B
+        st = {}
 
-        def stage1(i, g, m, add_eng):
+        def mm1(i, g, m):
             codes, scales = vq[i, g]
-            pa = psum.tile([P, H], F32, name="pa", tag="pa", bufs=2)
-            pg = psum.tile([P, H], F32, name="pg", tag="pg", bufs=2)
+            pg = psum.tile([P, H], F32, name="pg", tag="pm", bufs=4)
+            pa = psum.tile([P, H], F32, name="pa", tag="pm", bufs=4)
             for k, bank in ((1, pg), (0, pa)):
                 nc.tensor.matmul_mx(
                     out=bank[:],
@@ -126,57 +168,80 @@ def tile_patch_channel_mixer_f3_kernel(tc, x, alpha, beta, wa, ba, wg, bg, gamma
                 )
             sg = work.tile([P, T, P], F32, name="sg", tag="sg", bufs=3)
             nc.scalar.activation(
-                out=sg[:], in_=pg[:].rearrange("p (q t) -> p t q", t=T), func=ACT.Sigmoid, bias=col(3, m)
+                out=sg[:], in_=pg[:].rearrange("p (q t) -> p t q", t=T), func=ACT.Sigmoid, bias=col(3, m),
             )
-            tt = work.tile([P, T, P], F32, name="tt", tag="tt", bufs=3)
-            nc.vector.scalar_tensor_tensor(
-                out=tt[:], in0=pa[:].rearrange("p (q t) -> p t q", t=T), scalar=col(2, m), in1=sg[:],
-                op0=ALU.add, op1=ALU.mult,
-            )
+            st[i, g, m] = (pa, sg)
+
+        def mul1(i, g, m):
+            pa, sg = st[i, g, m]
             if us[i] is None:
                 us[i] = work.tile([P, T, G, T, P], F32, name="u", tag="u", bufs=4)
-            xin = xs[i][:, m, g * H : (g + 1) * H].rearrange("p (q t) -> p t q", t=T)
-            eng = nc.gpsimd if add_eng == "g" else nc.vector
-            eng.tensor_tensor(out=us[i][:, m, g, :, :], in0=tt[:], in1=xin, op=ALU.add)
+            nc.vector.scalar_tensor_tensor(
+                out=us[i][:, m, g, :, :], in0=pa[:].rearrange("p (q t) -> p t q", t=T), scalar=col(2, m), in1=sg[:],
+                op0=ALU.add, op1=ALU.mult,
+            )
 
+        def add1(i, g, m):
+            xin = xs[i][:, m, g * H : (g + 1) * H].rearrange("p (q t) -> p t q", t=T)
+            if NAT[m] == "g":
+                ux[i, g, m] = work.tile([P, T, P], F32, name="ux", tag="ux", bufs=2)
+                nc.gpsimd.tensor_tensor(out=ux[i, g, m][:], in0=us[i][:, m, g, :, :], in1=xin, op=ALU.add)
+            elif NAT[m] == "v":
+                nc.vector.tensor_tensor(out=us[i][:, m, g, :, :], in0=us[i][:, m, g, :, :], in1=xin, op=ALU.add)
+
+        ux = {}
         has = {}
 
-        def trans_h(i, g, copy_eng):
-            ha = work.tile([P, T, H], BF16, name="ha", tag="ha", bufs=2)
-            for t in range(T):
-                bank = psum.tile([P, T, P], F32, name="pt", tag="pt", bufs=4)
-                for m in range(T):
-                    nc.tensor.transpose(bank[:, m, :], us[i][:, m, g, t, :], ident[:])
-                q = g * T + t
-                if copy_eng[t] == "s":
-                    nc.scalar.activation(
-                        out=ha[:, t, :], in_=bank[:].rearrange("p m c -> p (m c)"), func=ACT.Identity,
-                        scale=dcol(0, q), bias=dcol(1, q),
-                    )
-                else:
-                    nc.vector.tensor_scalar(
-                        out=ha[:, t, :], in0=bank[:].rearrange("p m c -> p (m c)"),
-                        scalar1=dcol(0, q), scalar2=dcol(1, q), op0=ALU.mult, op1=ALU.add,
-                    )
-            has[i, g] = ha
+        def trans_h(i, g, t, eng):
+            if t == 0:
+                has[i, g] = work.tile([P, T, H], BF16, name="ha", tag="ha", bufs=2)
+            bank = psum.tile([P, T, P], F32, name="pt", tag="pt", bufs=4)
+            for m in range(T):
+                xin = xs[i][:, m, g * H : (g + 1) * H].rearrange("p (q t) -> p t q", t=T)[:, t, :]
+                nc.tensor.matmul(bank[:, m, :], lhsT=xin, rhs=ident_bf[:], start=(m == 0), stop=False)
+            for m in range(T):
+                nc.tensor.matmul(
+                    bank[:, m, :], lhsT=us[i][:, m, g, t, :], rhs=ident[:], is_transpose=True,
+                    start=False, stop=(m == T - 1),
+                )
+            q = g * T + t
+            if eng == "s":
+                nc.scalar.activation(
+                    out=has[i, g][:, t, :], in_=bank[:].rearrange("p m c -> p (m c)"), func=ACT.Identity,
+                    scale=dcol(0, q), bias=dcol(1, q),
+                )
+            else:
+                nc.vector.tensor_scalar(
+                    out=has[i, g][:, t, :], in0=bank[:].rearrange("p m c -> p (m c)"),
+                    scalar1=dcol(0, q), scalar2=dcol(1, q), op0=ALU.mult, op1=ALU.add,
+                )
 
+        hin = {}
         hq = {}
 
+        def inter_h(i, g, part, parts, eng="v"):
+            if part == 0:
+                hin[i, g] = work.tile([P, H * T], BF16, name="inter", tag="inter", bufs=5, align_bytes=64)
+            w = H // parts
+            lo = part * w
+            d = hin[i, g][:, lo * T : (lo + w) * T].rearrange("p (c k t) -> p c t k", k=4, t=T)
+            s = has[i, g][:, :, lo : lo + w].rearrange("p t (c k) -> p c t k", k=4)
+            if eng == "s":
+                nc.scalar.copy(out=d, in_=s)
+            else:
+                nc.vector.tensor_copy(out=d, in_=s)
+
         def quant_h(i, g):
-            inter = work.tile([P, H * T], BF16, name="inter", tag="inter", bufs=4, align_bytes=64)
-            nc.vector.tensor_copy(
-                out=inter[:].rearrange("p (c t) -> p c t", t=T), in_=has[i, g][:].rearrange("p t c -> p c t")
-            )
-            codes = work.tile([P, H], U32, name="h_codes", tag="h_codes", bufs=8, align_bytes=64)
-            scales = work.tile([P, H], U8, name="h_scales", tag="h_scales", bufs=8, align_bytes=64)
-            quant(inter[:], codes[:], scales[:], E5M2)
+            codes = work.tile([P, H], U32, name="h_codes", tag="h_codes", bufs=6, align_bytes=64)
+            scales = work.tile([P, H], U8, name="h_scales", tag="h_scales", bufs=6, align_bytes=64)
+            quant(hin[i, g][:], codes[:], scales[:], E5M2)
             hq[i, g] = (codes, scales)
 
         ges = {}
 
         def stage2(i, f, t):
             q = f * T + t
-            bank = psum.tile([P, H], F32, name="pz", tag="pa" if t % 2 else "pg", bufs=2)
+            bank = psum.tile([P, H], F32, name="pz", tag="pm", bufs=4)
             for g in range(G):
                 codes, scales = hq[i, g]
                 nc.tensor.matmul_mx(
@@ -190,35 +255,53 @@ def tile_patch_channel_mixer_f3_kernel(tc, x, alpha, beta, wa, ba, wg, bg, gamma
             nc.scalar.activation(out=ge[:], in_=bank[:], func=ACT.Gelu_apprx_tanh, bias=dcol(2, q))
             ges[i, f, t] = ge
 
-        def finish(i, f):
-            res = work.tile([P, T, H], F32, name="res", tag="res", bufs=2)
-            ov = out[i].rearrange("(p t) d -> p t d", t=T)
-            for m in range(T):
-                bank = psum.tile([P, T, P], F32, name="pt", tag="pt", bufs=4)
-                for t in range(T):
-                    nc.tensor.transpose(bank[:, t, :], ges[i, f, t][:, m * P : (m + 1) * P], ident[:])
-                nc.vector.tensor_tensor(
-                    out=res[:, m, :].rearrange("p (q t) -> p q t", t=T),
-                    in0=bank[:].rearrange("p t q -> p q t"),
-                    in1=us[i][:, m, f, :, :].rearrange("p t q -> p q t"),
-                    op=ALU.add,
-                )
-                if m % 2:
-                    nc.sync.dma_start(
-                        out=ov[:, m - 1 : m + 1, f * H : (f + 1) * H], in_=res[:, m - 1 : m + 1, :]
-                    )
+        banks = {}
+        res = {}
 
-        for i in range(1, B - 1):
-            pass
-        affine_v(0, (0,))
-        for k in range(2):
-            weight_block(raws[k], w_codes[:, k, :], w_scales[:, k, :], "sv"[k])
-        quant_v(0, 0, "v")
+        def trans_o(i, f, m):
+            bank = psum.tile([P, T, P], F32, name="pt", tag="pt", bufs=4)
+            if NAT[m] == "p":
+                nc.tensor.matmul(
+                    bank[:].rearrange("p t q -> p (t q)"), lhsT=ident_bf[:], rhs=xs[i][:, m, f * H : (f + 1) * H],
+                    start=True, stop=False,
+                )
+            for t in range(T):
+                nc.tensor.matmul(
+                    bank[:, t, :], lhsT=ges[i, f, t][:, m * P : (m + 1) * P], rhs=ident[:], is_transpose=True,
+                    start=(NAT[m] != "p"), stop=(NAT[m] != "p" or t == T - 1),
+                )
+            banks[i, f, m] = bank
+
+        def final(i, f, m):
+            if m == 0:
+                res[i, f] = work.tile([P, T, H], F32, name="res", tag="res", bufs=2)
+            r = res[i, f]
+            nc.vector.tensor_tensor(
+                out=r[:, m, :].rearrange("p (q t) -> p q t", t=T),
+                in0=banks[i, f, m][:].rearrange("p a b -> p (a b)").rearrange("p (q t) -> p q t", t=T),
+                in1=(ux[i, f, m][:] if NAT[m] == "g" else us[i][:, m, f, :, :]).rearrange("p t q -> p q t"),
+                op=ALU.add,
+            )
+            if m % 2:
+                ov = out[i].rearrange("(p t) d -> p t d", t=T)
+                nc.sync.dma_start(
+                    out=ov[:, m - 1 : m + 1, f * H : (f + 1) * H], in_=r[:, m - 1 : m + 1, :]
+                )
+
+        weight_block(raws[0], w_codes[:, 1, :], w_scales[:, 1, :], HW)
+        for t in range(T):
+            affine_v(0, t, 0, H)
+        for part in range(4):
+            inter_v(0, 0, part, 4, V0[part])
+        quant_v(0, 0)
+        weight_block(raws[1], w_codes[:, 0, :], w_scales[:, 0, :], HW)
+        for t in range(T):
+            affine_v(0, t, H, D)
+        inter_v(0, 1, 0, 1, "s")
+        quant_v(0, 1)
+
         load_x(1)
         nc.sync.dma_start(out=xs[1][:], in_=xv[1])
-        affine_v(0, (1,))
-        quant_v(0, 1, "v")
-
         wc_raw = []
         for g in range(G):
             for f in range(G):
@@ -228,31 +311,67 @@ def tile_patch_channel_mixer_f3_kernel(tc, x, alpha, beta, wa, ba, wg, bg, gamma
                 wc_raw.append((g, f, raw))
 
         units = [(i, g) for i in range(B) for g in range(G)]
-        for n, (i, g) in enumerate(units):
-            if g == 0 and i + 2 < B:
-                load_x(i + 2)
-                nc.sync.dma_start(out=xs[i + 2][:], in_=xv[i + 2])
-            if g == 0 and i + 1 < B:
-                affine_v(i + 1, (0, 1))
-            for m in range(T):
-                stage1(i, g, m, "v")
-                if m == 1 and i + 1 < B:
-                    quant_v(i + 1, g, "s")
-            if n < 4:
-                cg, cf, raw = wc_raw[n]
-                weight_block(
-                    raw, c_codes[:, cg, cf * H : (cf + 1) * H], c_scales[:, cg, cf * H : (cf + 1) * H], "v"
-                )
-            if n >= 1:
-                trans_h(*units[n - 1], "ssss")
-            if n >= 2:
-                quant_h(*units[n - 2])
-        trans_h(*units[-1], "svsv")
-        quant_h(*units[-2])
-        quant_h(*units[-1])
-        for n, (i, f) in enumerate(units):
-            for t in range(T):
-                stage2(i, f, t)
-            if n >= 1:
-                finish(*units[n - 1])
-        finish(*units[-1])
+        n_steps = B * G * T
+
+        def at(s, lag):
+            r = s - lag
+            if 0 <= r < n_steps:
+                return units[r // T] + (r % T,)
+            return None
+
+        def run(s, lag, fn):
+            k = at(s, lag)
+            if k:
+                fn(*k)
+
+        with tc.manual_schedule(engines=MAN):
+            for s in range(0, n_steps + L_OT + 2, R):
+                two = range(s, s + R)
+                for e in two:
+                    k = at(e, 0)
+                    if k:
+                        i, g, m = k
+                        if g == 0 and m == 0 and i + 2 < B:
+                            load_x(i + 2)
+                            nc.sync.dma_start(out=xs[i + 2][:], in_=xv[i + 2])
+                        mm1(i, g, m)
+                for e in two:
+                    run(e, L_Z, stage2)
+                for e in two:
+                    run(e, L_M, mul1)
+                for e in two:
+                    run(e, L_HT, lambda i, g, m: trans_h(i, g, m, HC[m]))
+                for e in two:
+                    run(e, L_OT, trans_o)
+                for e in two:
+                    run(e, L_OT, final)
+                for e in two:
+                    run(e, L_OT - 6, add1)
+                for e in two:
+                    k = at(e, 0)
+                    if k and k[0] + 1 < B:
+                        if k[1] == 0:
+                            affine_v(k[0] + 1, k[2])
+                for e in two:
+                    k = at(e, 4)
+                    if k and k[0] + 1 < B:
+                        inter_v(k[0] + 1, k[1], k[2], 4, VI[k[2]])
+                        if k[2] == 3:
+                            quant_v(k[0] + 1, k[1])
+                for e in two:
+                    k = at(e, L_HI)
+                    if k:
+                        if k[2] % (4 // HP) == 0:
+                            inter_h(k[0], k[1], k[2] // (4 // HP), HP, HI[k[2]])
+                        if k[2] == 3:
+                            quant_h(k[0], k[1])
+                for e in two:
+                    r = e - WC_AT
+                    if 0 <= r < 16:
+                        cg, cf, raw = wc_raw[r // 4]
+                        weight_part(("c", r // 4), raw, r % 4, WC_ENG[r % 4], True)
+                        if r % 4 == 3:
+                            weight_quant(
+                                ("c", r // 4), c_codes[:, cg, cf * H : (cf + 1) * H],
+                                c_scales[:, cg, cf * H : (cf + 1) * H],
+                            )

@@ -18,17 +18,18 @@ E5M2 = mybir.dt.float8_e5m2_x4
 ALU = mybir.AluOpType
 ACT = mybir.ActivationFunctionType
 
-L_OT = 40
-L_Z = 36
+L_OT = 32
+L_Z = 28
 L_M = 0
 L_HI = 8
 R = 4
-MAN = {mybir.EngineType.PE}
+MAN = {mybir.EngineType.SP}
 WC_ENG = "vvvv"
-NAT = "vvvv"
+NAT = "vgvg"
 WC_AT = 1
 HI = "vvvv"
 HP = 2
+SG = False
 HW = "vsvs"
 V0 = "vsvv"
 L_HT = 4
@@ -142,6 +143,8 @@ def tile_patch_channel_mixer_f3_kernel(tc, x, alpha, beta, wa, ba, wg, bg, gamma
             s = vas[i][:, :, g * H + lo : g * H + lo + w].rearrange("p t (c k) -> p c t k", k=4)
             if eng == "s":
                 nc.scalar.copy(out=d, in_=s)
+            elif eng == "g":
+                nc.gpsimd.tensor_scalar(out=d, in0=s, scalar1=1.0, scalar2=0.0, op0=ALU.mult, op1=ALU.add)
             else:
                 nc.vector.tensor_copy(out=d, in_=s)
 
@@ -183,7 +186,9 @@ def tile_patch_channel_mixer_f3_kernel(tc, x, alpha, beta, wa, ba, wg, bg, gamma
 
         def add1(i, g, m):
             xin = xs[i][:, m, g * H : (g + 1) * H].rearrange("p (q t) -> p t q", t=T)
-            if NAT[m] == "g":
+            if NAT[m] == "G":
+                nc.gpsimd.tensor_tensor(out=us[i][:, m, g, :, :], in0=us[i][:, m, g, :, :], in1=xin, op=ALU.add)
+            elif NAT[m] == "g":
                 ux[i, g, m] = work.tile([P, T, P], F32, name="ux", tag="ux", bufs=2)
                 nc.gpsimd.tensor_tensor(out=ux[i, g, m][:], in0=us[i][:, m, g, :, :], in1=xin, op=ALU.add)
             elif NAT[m] == "v":
@@ -197,8 +202,10 @@ def tile_patch_channel_mixer_f3_kernel(tc, x, alpha, beta, wa, ba, wg, bg, gamma
                 has[i, g] = work.tile([P, T, H], BF16, name="ha", tag="ha", bufs=2)
             bank = psum.tile([P, T, P], F32, name="pt", tag="pt", bufs=4)
             for m in range(T):
+                if NAT[m] == "G":
+                    continue
                 xin = xs[i][:, m, g * H : (g + 1) * H].rearrange("p (q t) -> p t q", t=T)[:, t, :]
-                nc.tensor.matmul(bank[:, m, :], lhsT=xin, rhs=ident_bf[:], start=(m == 0), stop=False)
+                nc.tensor.matmul(bank[:, m, :], lhsT=xin, rhs=ident_bf[:], start=(m == NAT.count("G")), stop=False)
             for m in range(T):
                 nc.tensor.matmul(
                     bank[:, m, :], lhsT=us[i][:, m, g, t, :], rhs=ident[:], is_transpose=True,
@@ -276,7 +283,12 @@ def tile_patch_channel_mixer_f3_kernel(tc, x, alpha, beta, wa, ba, wg, bg, gamma
             if m == 0:
                 res[i, f] = work.tile([P, T, H], F32, name="res", tag="res", bufs=2)
             r = res[i, f]
-            nc.vector.tensor_tensor(
+            if NAT[m] == "p" and SG:
+                nc.scalar.copy(out=r[:, m, :], in_=banks[i, f, m][:].rearrange("p a b -> p (a b)"))
+                rv = r[:, m, :].rearrange("p (q t) -> p q t", t=T)
+                nc.gpsimd.tensor_tensor(out=rv, in0=rv, in1=us[i][:, m, f, :, :].rearrange("p t q -> p q t"), op=ALU.add)
+            else:
+              nc.vector.tensor_tensor(
                 out=r[:, m, :].rearrange("p (q t) -> p q t", t=T),
                 in0=banks[i, f, m][:].rearrange("p a b -> p (a b)").rearrange("p (q t) -> p q t", t=T),
                 in1=(ux[i, f, m][:] if NAT[m] == "g" else us[i][:, m, f, :, :]).rearrange("p t q -> p q t"),
@@ -339,6 +351,7 @@ def tile_patch_channel_mixer_f3_kernel(tc, x, alpha, beta, wa, ba, wg, bg, gamma
                     run(e, L_Z, stage2)
                 for e in two:
                     run(e, L_M, mul1)
+                    run(e, L_M, lambda i, g, m: NAT[m] == "G" and add1(i, g, m))
                 for e in two:
                     run(e, L_HT, lambda i, g, m: trans_h(i, g, m, HC[m]))
                 for e in two:
@@ -346,7 +359,7 @@ def tile_patch_channel_mixer_f3_kernel(tc, x, alpha, beta, wa, ba, wg, bg, gamma
                 for e in two:
                     run(e, L_OT, final)
                 for e in two:
-                    run(e, L_OT - 6, add1)
+                    run(e, L_OT - 6, lambda i, g, m: NAT[m] != "G" and add1(i, g, m))
                 for e in two:
                     k = at(e, 0)
                     if k and k[0] + 1 < B:

from contextlib import ExitStack

import concourse.mybir as mybir
from concourse.masks import make_identity

B, NP, D = 4, 512, 1024
P = 128
T = 4
H = 512
G = D // H

F32 = mybir.dt.float32
BF16 = mybir.dt.bfloat16
U32 = mybir.dt.uint32
U8 = mybir.dt.uint8
E4M3 = mybir.dt.float8_e4m3fn_x4
E5M2 = mybir.dt.float8_e5m2_x4
ALU = mybir.AluOpType
ACT = mybir.ActivationFunctionType

L_OT = 32
L_Z = 28
L_M = 0
L_HI = 8
R = 4
MAN = {mybir.EngineType.SP}
WC_ENG = "vvvv"
NAT = "vgvg"
WC_AT = 1
HI = "vvvv"
HP = 2
SG = False
HW = "vsvs"
V0 = "vsvv"
L_HT = 4
VI = "sssv"
HC = "ssss"
FLOPS = 2 * 2 * B * D * NP * NP + 2 * B * NP * D * D


def tile_patch_channel_mixer_f3_kernel(tc, x, alpha, beta, wa, ba, wg, bg, gamma, delta, wc, bc, out):
    nc = tc.nc
    with ExitStack() as ctx:
        keep = ctx.enter_context(tc.tile_pool(name="keep", bufs=1))
        work = ctx.enter_context(tc.tile_pool(name="work", bufs=2))
        psum = ctx.enter_context(tc.psum_pool(name="psum", bufs=1))

        par_p = keep.tile([P, 4, 16], BF16, name="par_p")
        par_d = keep.tile([P, 2, 16], BF16, name="par_d")
        for s, vec in enumerate((alpha, beta, ba, bg)):
            nc.scalar.dma_start(out=par_p[:, s, 0:T], in_=vec.rearrange("(p t) -> p t", t=T))
        bc_rows = keep.tile([P, P], BF16, name="bc_rows", align_bytes=64)
        nc.gpsimd.memset(bc_rows[:], 0.0)
        nc.scalar.dma_start(out=bc_rows[0 : G * T, :], in_=bc.rearrange("(q p) -> q p", p=P))
        for s, vec in enumerate((gamma, delta)):
            nc.scalar.dma_start(
                out=par_d[:, s, 0 : G * T].rearrange("p (g t) -> p g t", t=T),
                in_=vec.rearrange("(g p t) -> p g t", g=G, t=T),
            )
        xs = [None] * B

        def load_x(i):
            xs[i] = work.tile([P, T, D], BF16, name="x_sb", tag="x_sb", bufs=4)
            return xs[i]

        x0 = load_x(0)
        xv = [x[i].rearrange("(p t) d -> p t d", t=T) for i in range(B)]
        raws = []
        for w in (wg, wa):
            raw = work.tile([P, T, NP], BF16, name="raw", tag="raw", bufs=3)
            nc.sync.dma_start(out=raw[:], in_=w.rearrange("(p j) c -> p j c", j=T))
            raws.append(raw)
            if w is wg:
                nc.sync.dma_start(out=x0[:, :, 0:H], in_=xv[0][:, :, 0:H])
        nc.sync.dma_start(out=x0[:, :, H:D], in_=xv[0][:, :, H:D])

        ident = keep.tile([P, P], F32, name="ident")
        make_identity(nc, ident[:])
        ident_bf = keep.tile([P, P], BF16, name="ident_bf")
        make_identity(nc, ident_bf[:])
        pp = keep.tile([P, 4, T], F32, name="pp")
        pd = keep.tile([P, 3, G * T], F32, name="pd")
        nc.vector.tensor_copy(out=pp[:], in_=par_p[:, :, 0:T])
        nc.vector.tensor_copy(out=pd[:, 0:2, :], in_=par_d[:, :, 0 : G * T])
        bc_t = psum.tile([P, P], BF16, name="bc_t", tag="pt", bufs=4)
        nc.tensor.transpose(bc_t[:], bc_rows[:], ident_bf[:])
        nc.vector.tensor_copy(out=pd[:, 2, :], in_=bc_t[:, 0 : G * T])

        def col(s, t):
            return pp[:, s, t : t + 1]

        def dcol(s, q):
            return pd[:, s, q : q + 1]

        def quant(src, codes, scales, fmt):
            nc.vector.quantize_mx(out=codes.bitcast(fmt), scales=scales, in_=src)

        winter = {}

        def weight_part(key, raw, t, eng, natural=False):
            if t == 0:
                winter[key] = work.tile([P, H * T], BF16, name="inter", tag="inter", bufs=5, align_bytes=64)
            d = winter[key][:].rearrange("p (t m j) -> p t m j", t=T, j=T)[:, t]
            s = raw[:].rearrange("p j (t m) -> p t m j" if natural else "p j (m t) -> p t m j", t=T)[:, t]
            if eng == "s":
                nc.scalar.copy(out=d, in_=s)
            elif eng == "g":
                nc.gpsimd.tensor_scalar(out=d, in0=s, scalar1=1.0, scalar2=0.0, op0=ALU.mult, op1=ALU.add)
            else:
                nc.vector.tensor_copy(out=d, in_=s)

        def weight_quant(key, codes, scales):
            quant(winter[key][:], codes, scales, E4M3)

        def weight_block(raw, codes, scales, eng):
            for t in range(T):
                weight_part("w", raw, t, eng[t])
            weight_quant("w", codes, scales)

        w_codes = keep.tile([P, 2, NP], U32, name="w_codes", align_bytes=64)
        w_scales = keep.tile([P, 2, NP], U8, name="w_scales", align_bytes=64)
        c_codes = keep.tile([P, G, D], U32, name="c_codes", align_bytes=64)
        c_scales = keep.tile([P, G, D], U8, name="c_scales", align_bytes=64)

        vas = [None] * B
        vin = {}
        vq = {}

        def affine_v(i, t, lo=0, hi=D):
            if vas[i] is None:
                vas[i] = work.tile([P, T, D], BF16, name="va", tag="va", bufs=2)
            nc.vector.tensor_scalar(
                out=vas[i][:, t, lo:hi], in0=xs[i][:, t, lo:hi],
                scalar1=col(0, t), scalar2=col(1, t), op0=ALU.mult, op1=ALU.add,
            )

        def inter_v(i, g, part, parts, eng):
            if part == 0:
                vin[i, g] = work.tile([P, H * T], BF16, name="inter", tag="inter", bufs=5, align_bytes=64)
            w = H // parts
            lo = part * w
            d = vin[i, g][:, lo * T : (lo + w) * T].rearrange("p (c k t) -> p c t k", k=4, t=T)
            s = vas[i][:, :, g * H + lo : g * H + lo + w].rearrange("p t (c k) -> p c t k", k=4)
            if eng == "s":
                nc.scalar.copy(out=d, in_=s)
            elif eng == "g":
                nc.gpsimd.tensor_scalar(out=d, in0=s, scalar1=1.0, scalar2=0.0, op0=ALU.mult, op1=ALU.add)
            else:
                nc.vector.tensor_copy(out=d, in_=s)

        def quant_v(i, g):
            codes = work.tile([P, H], U32, name="v_codes", tag="v_codes", bufs=3, align_bytes=64)
            scales = work.tile([P, H], U8, name="v_scales", tag="v_scales", bufs=3, align_bytes=64)
            quant(vin[i, g][:], codes[:], scales[:], E4M3)
            vq[i, g] = (codes, scales)

        us = [None] * B
        st = {}

        def mm1(i, g, m):
            codes, scales = vq[i, g]
            pg = psum.tile([P, H], F32, name="pg", tag="pm", bufs=4)
            pa = psum.tile([P, H], F32, name="pa", tag="pm", bufs=4)
            for k, bank in ((1, pg), (0, pa)):
                nc.tensor.matmul_mx(
                    out=bank[:],
                    lhsT=w_codes[:, k, m * P : (m + 1) * P].bitcast(E4M3),
                    lhsT_scale=w_scales[:, k, m * P : (m + 1) * P],
                    rhs=codes[:].bitcast(E4M3), rhs_scale=scales[:],
                    start=True, stop=True,
                )
            sg = work.tile([P, T, P], F32, name="sg", tag="sg", bufs=3)
            nc.scalar.activation(
                out=sg[:], in_=pg[:].rearrange("p (q t) -> p t q", t=T), func=ACT.Sigmoid, bias=col(3, m),
            )
            st[i, g, m] = (pa, sg)

        def mul1(i, g, m):
            pa, sg = st[i, g, m]
            if us[i] is None:
                us[i] = work.tile([P, T, G, T, P], F32, name="u", tag="u", bufs=4)
            nc.vector.scalar_tensor_tensor(
                out=us[i][:, m, g, :, :], in0=pa[:].rearrange("p (q t) -> p t q", t=T), scalar=col(2, m), in1=sg[:],
                op0=ALU.add, op1=ALU.mult,
            )

        def add1(i, g, m):
            xin = xs[i][:, m, g * H : (g + 1) * H].rearrange("p (q t) -> p t q", t=T)
            if NAT[m] == "G":
                nc.gpsimd.tensor_tensor(out=us[i][:, m, g, :, :], in0=us[i][:, m, g, :, :], in1=xin, op=ALU.add)
            elif NAT[m] == "g":
                ux[i, g, m] = work.tile([P, T, P], F32, name="ux", tag="ux", bufs=2)
                nc.gpsimd.tensor_tensor(out=ux[i, g, m][:], in0=us[i][:, m, g, :, :], in1=xin, op=ALU.add)
            elif NAT[m] == "v":
                nc.vector.tensor_tensor(out=us[i][:, m, g, :, :], in0=us[i][:, m, g, :, :], in1=xin, op=ALU.add)

        ux = {}
        has = {}

        def trans_h(i, g, t, eng):
            if t == 0:
                has[i, g] = work.tile([P, T, H], BF16, name="ha", tag="ha", bufs=2)
            bank = psum.tile([P, T, P], F32, name="pt", tag="pt", bufs=4)
            for m in range(T):
                if NAT[m] == "G":
                    continue
                xin = xs[i][:, m, g * H : (g + 1) * H].rearrange("p (q t) -> p t q", t=T)[:, t, :]
                nc.tensor.matmul(bank[:, m, :], lhsT=xin, rhs=ident_bf[:], start=(m == NAT.count("G")), stop=False)
            for m in range(T):
                nc.tensor.matmul(
                    bank[:, m, :], lhsT=us[i][:, m, g, t, :], rhs=ident[:], is_transpose=True,
                    start=False, stop=(m == T - 1),
                )
            q = g * T + t
            if eng == "s":
                nc.scalar.activation(
                    out=has[i, g][:, t, :], in_=bank[:].rearrange("p m c -> p (m c)"), func=ACT.Identity,
                    scale=dcol(0, q), bias=dcol(1, q),
                )
            else:
                nc.vector.tensor_scalar(
                    out=has[i, g][:, t, :], in0=bank[:].rearrange("p m c -> p (m c)"),
                    scalar1=dcol(0, q), scalar2=dcol(1, q), op0=ALU.mult, op1=ALU.add,
                )

        hin = {}
        hq = {}

        def inter_h(i, g, part, parts, eng="v"):
            if part == 0:
                hin[i, g] = work.tile([P, H * T], BF16, name="inter", tag="inter", bufs=5, align_bytes=64)
            w = H // parts
            lo = part * w
            d = hin[i, g][:, lo * T : (lo + w) * T].rearrange("p (c k t) -> p c t k", k=4, t=T)
            s = has[i, g][:, :, lo : lo + w].rearrange("p t (c k) -> p c t k", k=4)
            if eng == "s":
                nc.scalar.copy(out=d, in_=s)
            else:
                nc.vector.tensor_copy(out=d, in_=s)

        def quant_h(i, g):
            codes = work.tile([P, H], U32, name="h_codes", tag="h_codes", bufs=6, align_bytes=64)
            scales = work.tile([P, H], U8, name="h_scales", tag="h_scales", bufs=6, align_bytes=64)
            quant(hin[i, g][:], codes[:], scales[:], E5M2)
            hq[i, g] = (codes, scales)

        ges = {}

        def stage2(i, f, t):
            q = f * T + t
            bank = psum.tile([P, H], F32, name="pz", tag="pm", bufs=4)
            for g in range(G):
                codes, scales = hq[i, g]
                nc.tensor.matmul_mx(
                    out=bank[:],
                    lhsT=c_codes[:, g, q * P : (q + 1) * P].bitcast(E4M3),
                    lhsT_scale=c_scales[:, g, q * P : (q + 1) * P],
                    rhs=codes[:].bitcast(E5M2), rhs_scale=scales[:],
                    start=(g == 0), stop=(g == G - 1),
                )
            ge = work.tile([P, H], F32, name="ge", tag="ge", bufs=8)
            nc.scalar.activation(out=ge[:], in_=bank[:], func=ACT.Gelu_apprx_tanh, bias=dcol(2, q))
            ges[i, f, t] = ge

        banks = {}
        res = {}

        def trans_o(i, f, m):
            bank = psum.tile([P, T, P], F32, name="pt", tag="pt", bufs=4)
            if NAT[m] == "p":
                nc.tensor.matmul(
                    bank[:].rearrange("p t q -> p (t q)"), lhsT=ident_bf[:], rhs=xs[i][:, m, f * H : (f + 1) * H],
                    start=True, stop=False,
                )
            for t in range(T):
                nc.tensor.matmul(
                    bank[:, t, :], lhsT=ges[i, f, t][:, m * P : (m + 1) * P], rhs=ident[:], is_transpose=True,
                    start=(NAT[m] != "p"), stop=(NAT[m] != "p" or t == T - 1),
                )
            banks[i, f, m] = bank

        def final(i, f, m):
            if m == 0:
                res[i, f] = work.tile([P, T, H], F32, name="res", tag="res", bufs=2)
            r = res[i, f]
            if NAT[m] == "p" and SG:
                nc.scalar.copy(out=r[:, m, :], in_=banks[i, f, m][:].rearrange("p a b -> p (a b)"))
                rv = r[:, m, :].rearrange("p (q t) -> p q t", t=T)
                nc.gpsimd.tensor_tensor(out=rv, in0=rv, in1=us[i][:, m, f, :, :].rearrange("p t q -> p q t"), op=ALU.add)
            else:
              nc.vector.tensor_tensor(
                out=r[:, m, :].rearrange("p (q t) -> p q t", t=T),
                in0=banks[i, f, m][:].rearrange("p a b -> p (a b)").rearrange("p (q t) -> p q t", t=T),
                in1=(ux[i, f, m][:] if NAT[m] == "g" else us[i][:, m, f, :, :]).rearrange("p t q -> p q t"),
                op=ALU.add,
            )
            if m % 2:
                ov = out[i].rearrange("(p t) d -> p t d", t=T)
                nc.sync.dma_start(
                    out=ov[:, m - 1 : m + 1, f * H : (f + 1) * H], in_=r[:, m - 1 : m + 1, :]
                )

        weight_block(raws[0], w_codes[:, 1, :], w_scales[:, 1, :], HW)
        for t in range(T):
            affine_v(0, t, 0, H)
        for part in range(4):
            inter_v(0, 0, part, 4, V0[part])
        quant_v(0, 0)
        weight_block(raws[1], w_codes[:, 0, :], w_scales[:, 0, :], HW)
        for t in range(T):
            affine_v(0, t, H, D)
        inter_v(0, 1, 0, 1, "s")
        quant_v(0, 1)

        load_x(1)
        nc.sync.dma_start(out=xs[1][:], in_=xv[1])
        wc_raw = []
        for g in range(G):
            for f in range(G):
                raw = work.tile([P, T, NP], BF16, name="raw", tag="raw", bufs=3)
                src = wc[g * H : (g + 1) * H, f * H : (f + 1) * H]
                nc.sync.dma_start(out=raw[:], in_=src.rearrange("(p j) c -> p j c", j=T))
                wc_raw.append((g, f, raw))

        units = [(i, g) for i in range(B) for g in range(G)]
        n_steps = B * G * T

        def at(s, lag):
            r = s - lag
            if 0 <= r < n_steps:
                return units[r // T] + (r % T,)
            return None

        def run(s, lag, fn):
            k = at(s, lag)
            if k:
                fn(*k)

        with tc.manual_schedule(engines=MAN):
            for s in range(0, n_steps + L_OT + 2, R):
                two = range(s, s + R)
                for e in two:
                    k = at(e, 0)
                    if k:
                        i, g, m = k
                        if g == 0 and m == 0 and i + 2 < B:
                            load_x(i + 2)
                            nc.sync.dma_start(out=xs[i + 2][:], in_=xv[i + 2])
                        mm1(i, g, m)
                for e in two:
                    run(e, L_Z, stage2)
                for e in two:
                    run(e, L_M, mul1)
                    run(e, L_M, lambda i, g, m: NAT[m] == "G" and add1(i, g, m))
                for e in two:
                    run(e, L_HT, lambda i, g, m: trans_h(i, g, m, HC[m]))
                for e in two:
                    run(e, L_OT, trans_o)
                for e in two:
                    run(e, L_OT, final)
                for e in two:
                    run(e, L_OT - 6, lambda i, g, m: NAT[m] != "G" and add1(i, g, m))
                for e in two:
                    k = at(e, 0)
                    if k and k[0] + 1 < B:
                        if k[1] == 0:
                            affine_v(k[0] + 1, k[2])
                for e in two:
                    k = at(e, 4)
                    if k and k[0] + 1 < B:
                        inter_v(k[0] + 1, k[1], k[2], 4, VI[k[2]])
                        if k[2] == 3:
                            quant_v(k[0] + 1, k[1])
                for e in two:
                    k = at(e, L_HI)
                    if k:
                        if k[2] % (4 // HP) == 0:
                            inter_h(k[0], k[1], k[2] // (4 // HP), HP, HI[k[2]])
                        if k[2] == 3:
                            quant_h(k[0], k[1])
                for e in two:
                    r = e - WC_AT
                    if 0 <= r < 16:
                        cg, cf, raw = wc_raw[r // 4]
                        weight_part(("c", r // 4), raw, r % 4, WC_ENG[r % 4], True)
                        if r % 4 == 3:
                            weight_quant(
                                ("c", r // 4), c_codes[:, cg, cf * H : (cf + 1) * H],
                                c_scales[:, cg, cf * H : (cf + 1) * H],
                            )
